import numpy as np
import ml_dtypes


def mxq(x, axis, fmt="e4m3"):
    dtype, down = {"e4m3": (ml_dtypes.float8_e4m3fn, 7), "e5m2": (ml_dtypes.float8_e5m2, 14)}[fmt]
    v = np.moveaxis(np.asarray(x, np.float32).astype(ml_dtypes.bfloat16).astype(np.float64), axis, -1)
    blocks = v.reshape(v.shape[:-1] + (-1, 32))
    amax = np.abs(blocks).max(-1, keepdims=True)
    byte = np.maximum(np.where(amax > 0, np.frexp(amax)[1] - 1 + 127, 0) - down, 1)
    scale = np.exp2(byte - 127.0)
    codes = (blocks / scale).astype(np.float32).astype(dtype).astype(np.float64)
    return np.moveaxis((codes * scale).reshape(v.shape), -1, axis)


WIDE = False


def mx_kscale(k):
    if not WIDE:
        return np.ones(k)
    levels = np.array([18, -18])
    if k % 512:
        return np.exp2(np.random.permutation(np.resize(levels, k // 32))).repeat(32)
    a = np.empty((k // 512, 16))
    for p in range(k // 512):
        a[p, :8] = np.random.permutation(np.resize(levels, 8))
        for g in range(8):
            far = levels[np.abs(levels - a[p, g]) >= 10]
            a[p, g + 8] = far[np.random.randint(len(far))]
    return np.exp2(a.ravel()).repeat(32)


def f64(x):
    return np.asarray(x).astype(np.float64)


def striped(idx):
    return np.tile(np.asarray(idx).reshape(-1, 16).T, (8, 1)).astype(np.uint16)


def unstriped(offs):
    return offs[:16].T.reshape(-1).astype(np.int64)


def setup_inputs():
    n = np.random.standard_normal
    uni = np.random.uniform
    px0 = np.random.randint(0, 2048, 512)
    px1 = (px0 + 1) % 2048
    px2 = (px0 + 64) % 2048
    px3 = (px0 + 65) % 2048
    f_e = mx_kscale(512)
    return {
        "xT": (n((512, 2048))).astype(np.float32),
        "W": (n((512, 512)) / np.sqrt(512) * f_e[:, None]).astype(np.float32),
        "dyT": (n((512, 512)) / f_e[:, None]).astype(np.float32),
        "fx": (uni(0.0, 1.0, (512, 1))).astype(np.float32),
        "fy": (uni(0.0, 1.0, (512, 1))).astype(np.float32),
        "offs0": striped(px0),
        "offs1": striped(px1),
        "offs2": striped(px2),
        "offs3": striped(px3),
    }


def reference(xT, W, dyT, fx, fy, offs0, offs1, offs2, offs3):
    px0 = unstriped(offs0)
    px1 = unstriped(offs1)
    px2 = unstriped(offs2)
    px3 = unstriped(offs3)
    dv = mxq(f64(dyT), 0, "e5m2").T @ mxq(f64(W), 0, "e4m3")
    xT_0 = f64(xT)[:, px0]
    t0 = xT_0.T
    xT_1 = f64(xT)[:, px1]
    t1 = xT_1.T
    xT_2 = f64(xT)[:, px2]
    t2 = xT_2.T
    xT_3 = f64(xT)[:, px3]
    t3 = xT_3.T
    hx = (1.0 - f64(fy)) * (t1 - t0) + f64(fy) * (t3 - t2)
    hy = (1.0 - f64(fx)) * (t2 - t0) + f64(fx) * (t3 - t1)
    gx = (dv * hx).sum(-1, keepdims=True)
    gy = (dv * hy).sum(-1, keepdims=True)
    out_0 = gx.T
    out_1 = gy.T
    return out_0, out_1

@@ -1,0 +1,162 @@
+from contextlib import ExitStack
+
+import concourse.mybir as mybir
+from concourse.masks import make_identity
+
+F32 = mybir.dt.float32
+BF16 = mybir.dt.bfloat16
+U32 = mybir.dt.uint32
+U16 = mybir.dt.uint16
+U8 = mybir.dt.uint8
+E4M3X4 = mybir.dt.float8_e4m3fn_x4
+E5M2X4 = mybir.dt.float8_e5m2_x4
+MULT = mybir.AluOpType.mult
+ADD = mybir.AluOpType.add
+COPY = mybir.ActivationFunctionType.Copy
+AXIS_X = mybir.AxisListType.X
+
+P = 128
+PACK = 4
+SAMPLES = 512
+FEATURES = 512
+PIXELS = 2048
+CORNERS = 4
+BLOCKS = 4
+FLOPS = 2 * 512 * 512 * 512
+
+
+def interleave(engine_copy, dst, src):
+    engine_copy(out=dst.rearrange("p (c i) t -> p c t i", i=4), in_=src.rearrange("p t (c i) -> p c t i", i=4))
+
+
+def tile_attend_gbilin_kernel(tc, xT, W, dyT, fx, fy, offs0, offs1, offs2, offs3, out_0, out_1):
+    nc = tc.nc
+    with ExitStack() as ctx:
+        keep = ctx.enter_context(tc.tile_pool(name="keep", bufs=1))
+        psum = ctx.enter_context(tc.psum_pool(name="psum", bufs=1))
+
+        w_rows = W.rearrange("(p t) d -> p t d", t=PACK)
+        dy_rows = dyT.rearrange("(p t) i -> p t i", t=PACK)
+        lists = [keep.tile([P, SAMPLES // 16], U16, name=f"list{c}") for c in range(CORNERS)]
+        image = [keep.tile([P, PIXELS], F32, name=f"image{b}") for b in range(BLOCKS)]
+        w_head = keep.tile([P, PACK, P], F32)
+        w_rest = keep.tile([P, PACK, 3 * P], F32)
+        dy_raw = [keep.tile([P, PACK, SAMPLES // 2], F32, name=f"dy_raw{h}") for h in range(2)]
+        f_rows = keep.tile([P, P], F32)
+        ident = keep.tile([P, P], F32)
+        grads = keep.tile([P, P], F32, align_bytes=64)
+
+        nc.sync.dma_start(out=w_head[:], in_=w_rows[:, :, 0:P])
+        for h in range(2):
+            nc.sync.dma_start(out=dy_raw[h][:], in_=dy_rows[:, :, h * 256:(h + 1) * 256])
+        nc.sync.dma_start(lists[0][:], offs0)
+        nc.sync.dma_start(out=image[0][:], in_=xT[0:P, :])
+        nc.sync.dma_start(lists[1][:], offs1)
+        nc.sync.dma_start(lists[2][:], offs2)
+        nc.sync.dma_start(lists[3][:], offs3)
+        nc.sync.dma_start(out=w_rest[:], in_=w_rows[:, :, P:])
+        for b in range(1, BLOCKS):
+            nc.sync.dma_start(out=image[b][:], in_=xT[b * P:(b + 1) * P, :])
+        nc.gpsimd.memset(f_rows[:], 0.0)
+        nc.gpsimd.memset(grads[:], 0.0)
+        make_identity(nc, ident[:])
+        nc.sync.dma_start(out=f_rows[0:4, :], in_=fx.rearrange("(s p) o -> s (p o)", p=P))
+        nc.sync.dma_start(out=f_rows[4:8, :], in_=fy.rearrange("(s p) o -> s (p o)", p=P))
+
+        w_codes = {}
+        w_scales = {}
+
+        def quantise_w(first, count, raw, engine_copy):
+            packed = keep.tile([P, count * P, PACK], BF16, name=f"w_packed{first}", align_bytes=64)
+            codes = keep.tile([P, count * P], U32, name=f"w_codes{first}", align_bytes=64)
+            scales = keep.tile([P, count * P], U8, name=f"w_scales{first}", align_bytes=64)
+            interleave(engine_copy, packed[:], raw)
+            nc.vector.quantize_mx(out=codes[:].bitcast(E4M3X4), scales=scales[:], in_=packed[:].rearrange("p d t -> p (d t)"))
+            for j in range(count):
+                w_codes[first + j] = codes[:, j * P:(j + 1) * P]
+                w_scales[first + j] = scales[:, j * P:(j + 1) * P]
+
+        quantise_w(0, 1, w_head[:], nc.scalar.copy)
+        dy_codes = keep.tile([P, SAMPLES], U32, align_bytes=64)
+        dy_scales = keep.tile([P, SAMPLES], U8, align_bytes=64)
+        split = 176
+        for h in range(2):
+            packed = keep.tile([P, 256, PACK], BF16, name=f"dy_packed{h}", align_bytes=64)
+            interleave(nc.vector.tensor_copy, packed[:, 0:split, :], dy_raw[h][:, :, 0:split])
+            interleave(nc.scalar.copy, packed[:, split:, :], dy_raw[h][:, :, split:])
+            cols = slice(h * 256, (h + 1) * 256)
+            nc.vector.quantize_mx(out=dy_codes[:, cols].bitcast(E5M2X4), scales=dy_scales[:, cols], in_=packed[:].rearrange("p i t -> p (i t)"))
+
+        dv = {}
+
+        def product(b):
+            bank = psum.tile([P, SAMPLES], F32, name="dv_bank", tag=f"dv_bank{b % 2}")
+            nc.tensor.matmul_mx(out=bank[:], lhsT=w_codes[b].bitcast(E4M3X4), lhsT_scale=w_scales[b],
+                                rhs=dy_codes[:].bitcast(E5M2X4), rhs_scale=dy_scales[:], start=True, stop=True)
+            dv[b] = keep.tile([P, SAMPLES], F32, name=f"dv{b}")
+            nc.scalar.copy(out=dv[b][:], in_=bank[:])
+
+        sums = keep.tile([P, BLOCKS, CORNERS], F32)
+        acc = [psum.tile([P, BLOCKS, P], F32, name=f"acc{c}") for c in range(CORNERS)]
+        acc_last = psum.tile([P, 2, P], F32)
+
+        def acc_of(c, s):
+            if c == CORNERS - 1 and s >= 2:
+                return acc_last[:, s - 2, :], s == 2, s == 3
+            last_s = 1 if c == CORNERS - 1 else 3
+            return acc[c][:, s, :], s == 0, s == last_s
+
+        def look_up(b, c, pieces):
+            terms = keep.tile([P, SAMPLES], F32, name=f"terms{b}{c}")
+            width = SAMPLES // pieces
+            for h in range(pieces):
+                cols = slice(h * width, (h + 1) * width)
+                offsets = lists[c][:, h * width // 16:(h + 1) * width // 16]
+                nc.vector.tensor_tensor(terms[:, cols], image[b][:].indirect(offsets), dv[b][:, cols], MULT)
+                for s in range(h * width // P, (h + 1) * width // P):
+                    target, first, last = acc_of(c, s)
+                    nc.tensor.matmul(out=target, lhsT=terms[:, s * P:(s + 1) * P], rhs=ident[:], is_transpose=True,
+                                     start=(b == 0 and first), stop=(b == BLOCKS - 1 and last))
+
+        def row_sums(c, blocks):
+            for s in blocks:
+                spent = keep.tile([P, P], F32, name="spent", tag="spent", bufs=2)
+                nc.scalar.activation(out=spent[:], in_=acc[c][:, s, :], func=COPY, accum_out=sums[:, s, c:c + 1])
+
+        product(0)
+        look_up(0, 0, 1)
+        quantise_w(1, 1, w_rest[:, :, 0:P], nc.scalar.copy)
+        product(1)
+        look_up(0, 1, 1)
+        look_up(0, 2, 1)
+        quantise_w(2, 2, w_rest[:, :, P:], nc.scalar.copy)
+        look_up(0, 3, 1)
+        product(2)
+        product(3)
+        for c in range(CORNERS):
+            look_up(1, c, 1)
+
+        f_bank = psum.tile([P, P], F32)
+        nc.tensor.transpose(f_bank[:], f_rows[:], ident[:])
+        weights = keep.tile([P, 2, BLOCKS, CORNERS], F32)
+        fx_cols, fy_cols = f_bank[:, 0:4], f_bank[:, 4:8]
+        for o, f_cols, signs in ((0, fy_cols, ((1.0, -1.0), (-1.0, 1.0), (-1.0, 0.0), (1.0, 0.0))),
+                                 (1, fx_cols, ((1.0, -1.0), (-1.0, 0.0), (-1.0, 1.0), (1.0, 0.0)))):
+            for c, (scale, bias) in enumerate(signs):
+                nc.scalar.activation(out=weights[:, o, :, c], in_=f_cols, func=COPY, scale=scale, bias=bias)
+
+        for c in range(CORNERS):
+            look_up(2, c, 1)
+            look_up(3, c, 2 if c == CORNERS - 1 else 1)
+            row_sums(c, range(2) if c == CORNERS - 1 else range(BLOCKS))
+        nc.vector.tensor_reduce(out=sums[:, 2:4, CORNERS - 1], in_=acc_last[:], axis=AXIS_X, op=ADD)
+
+        weighted = keep.tile([P, 2, BLOCKS, CORNERS], F32)
+        nc.vector.tensor_tensor(weighted[:], weights[:], sums[:].unsqueeze(1).to_broadcast([P, 2, BLOCKS, CORNERS]), MULT)
+        nc.vector.tensor_reduce(out=grads[:].rearrange("p (s r) -> p r s", r=32)[:, 0:2, :], in_=weighted[:], axis=AXIS_X, op=ADD)
+        turned = keep.tile([P, P], F32, align_bytes=64)
+        nc.vector.transpose(turned[:], grads[:])
+        nc.sync.dma_start(out=out_0.rearrange("o (s q r) -> (o q) s r", s=BLOCKS, q=4),
+                          in_=turned[0:P:32, :].rearrange("q (s r) -> q s r", r=32))
+        nc.scalar.dma_start(out=out_1.rearrange("o (s q r) -> (o q) s r", s=BLOCKS, q=4),
+                            in_=turned[1:P:32, :].rearrange("q (s r) -> q s r", r=32))

@@ -40,7 +40,8 @@ def tile_attend_gbilin_kernel(tc, xT, W, dyT, fx, fy, offs0, offs1, offs2, offs3
         lists = [keep.tile([P, SAMPLES // 16], U16, name=f"list{c}") for c in range(CORNERS)]
         image = [keep.tile([P, PIXELS], F32, name=f"image{b}") for b in range(BLOCKS)]
         w_head = keep.tile([P, PACK, P], F32)
-        w_rest = keep.tile([P, PACK, 3 * P], F32)
+        w_next = keep.tile([P, PACK, P], F32)
+        w_rest = keep.tile([P, PACK, 2 * P], F32, tag="w_rest")
         dy_raw = [keep.tile([P, PACK, SAMPLES // 2], F32, name=f"dy_raw{h}") for h in range(2)]
         f_rows = keep.tile([P, P], F32)
         ident = keep.tile([P, P], F32)
@@ -52,9 +53,10 @@ def tile_attend_gbilin_kernel(tc, xT, W, dyT, fx, fy, offs0, offs1, offs2, offs3
         nc.sync.dma_start(lists[0][:], offs0)
         nc.sync.dma_start(out=image[0][:], in_=xT[0:P, :])
         nc.sync.dma_start(lists[1][:], offs1)
+        nc.sync.dma_start(out=w_next[:], in_=w_rows[:, :, P:2 * P])
         nc.sync.dma_start(lists[2][:], offs2)
         nc.sync.dma_start(lists[3][:], offs3)
-        nc.sync.dma_start(out=w_rest[:], in_=w_rows[:, :, P:])
+        nc.sync.dma_start(out=w_rest[:], in_=w_rows[:, :, 2 * P:])
         for b in range(1, BLOCKS):
             nc.sync.dma_start(out=image[b][:], in_=xT[b * P:(b + 1) * P, :])
         nc.gpsimd.memset(f_rows[:], 0.0)
@@ -67,7 +69,7 @@ def tile_attend_gbilin_kernel(tc, xT, W, dyT, fx, fy, offs0, offs1, offs2, offs3
         w_scales = {}
 
         def quantise_w(first, count, raw, engine_copy):
-            packed = keep.tile([P, count * P, PACK], BF16, name=f"w_packed{first}", align_bytes=64)
+            packed = keep.tile([P, count * P, PACK], BF16, name=f"w_packed{first}", tag=f"w_packed{first}", align_bytes=64)
             codes = keep.tile([P, count * P], U32, name=f"w_codes{first}", align_bytes=64)
             scales = keep.tile([P, count * P], U8, name=f"w_scales{first}", align_bytes=64)
             interleave(engine_copy, packed[:], raw)
@@ -89,54 +91,57 @@ def tile_attend_gbilin_kernel(tc, xT, W, dyT, fx, fy, offs0, offs1, offs2, offs3
 
         dv = {}
 
-        def product(b):
+        def product(b, pieces=1):
             bank = psum.tile([P, SAMPLES], F32, name="dv_bank", tag=f"dv_bank{b % 2}")
             nc.tensor.matmul_mx(out=bank[:], lhsT=w_codes[b].bitcast(E4M3X4), lhsT_scale=w_scales[b],
                                 rhs=dy_codes[:].bitcast(E5M2X4), rhs_scale=dy_scales[:], start=True, stop=True)
-            dv[b] = keep.tile([P, SAMPLES], F32, name=f"dv{b}")
-            nc.scalar.copy(out=dv[b][:], in_=bank[:])
-
-        sums = keep.tile([P, BLOCKS, CORNERS], F32)
-        acc = [psum.tile([P, BLOCKS, P], F32, name=f"acc{c}") for c in range(CORNERS)]
-        acc_last = psum.tile([P, 2, P], F32)
-
-        def acc_of(c, s):
-            if c == CORNERS - 1 and s >= 2:
-                return acc_last[:, s - 2, :], s == 2, s == 3
-            last_s = 1 if c == CORNERS - 1 else 3
-            return acc[c][:, s, :], s == 0, s == last_s
-
-        def look_up(b, c, pieces):
-            terms = keep.tile([P, SAMPLES], F32, name=f"terms{b}{c}")
+            dv[b] = keep.tile([P, SAMPLES], F32, name=f"dv{b}", tag="w_rest" if b == 1 else f"dv{b}")
             width = SAMPLES // pieces
             for h in range(pieces):
-                cols = slice(h * width, (h + 1) * width)
-                offsets = lists[c][:, h * width // 16:(h + 1) * width // 16]
-                nc.vector.tensor_tensor(terms[:, cols], image[b][:].indirect(offsets), dv[b][:, cols], MULT)
-                for s in range(h * width // P, (h + 1) * width // P):
-                    target, first, last = acc_of(c, s)
-                    nc.tensor.matmul(out=target, lhsT=terms[:, s * P:(s + 1) * P], rhs=ident[:], is_transpose=True,
-                                     start=(b == 0 and first), stop=(b == BLOCKS - 1 and last))
+                nc.scalar.copy(out=dv[b][:, h * width:(h + 1) * width], in_=bank[:, h * width:(h + 1) * width])
+
+        sums = keep.tile([P, BLOCKS, CORNERS], F32)
+        last = CORNERS - 1
+        acc = [psum.tile([P, BLOCKS, P], F32, name=f"acc{c}") for c in range(CORNERS)]
+        acc_late = {s: psum.tile([P, P], F32, name=f"acc_late{s}") for s in (2, 3)}
+        terms = {}
+
+        def acc_of(c, s):
+            if c == last and s in acc_late:
+                return acc_late[s][:], True, True
+            return acc[c][:, s, :], s == 0, s == (1 if c == last else 3)
+
+        def look_up(b, c, s_from=0, s_to=BLOCKS, tag=None):
+            if (b, c) not in terms:
+                terms[b, c] = keep.tile([P, SAMPLES], F32, name=f"terms{b}{c}", tag=tag or f"terms{b}{c}", align_bytes=64)
+            cols = slice(s_from * P, s_to * P)
+            offsets = lists[c][:, s_from * P // 16:s_to * P // 16]
+            nc.vector.tensor_tensor(terms[b, c][:, cols], image[b][:].indirect(offsets), dv[b][:, cols], MULT)
+            for s in range(s_from, s_to):
+                target, opens, closes = acc_of(c, s)
+                nc.tensor.matmul(out=target, lhsT=terms[b, c][:, s * P:(s + 1) * P], rhs=ident[:], is_transpose=True,
+                                 start=(b == 0 and opens), stop=(b == BLOCKS - 1 and closes))
 
         def row_sums(c, blocks):
+            spent = keep.tile([P, BLOCKS, P], F32, name=f"spent{c}")
             for s in blocks:
-                spent = keep.tile([P, P], F32, name="spent", tag="spent", bufs=2)
-                nc.scalar.activation(out=spent[:], in_=acc[c][:, s, :], func=COPY, accum_out=sums[:, s, c:c + 1])
+                nc.scalar.activation(out=spent[:, s, :], in_=acc[c][:, s, :], func=COPY, accum_out=sums[:, s, c:c + 1])
 
-        product(0)
-        look_up(0, 0, 1)
-        quantise_w(1, 1, w_rest[:, :, 0:P], nc.scalar.copy)
+        product(0, 2)
+        look_up(0, 0, 0, 2)
+        look_up(0, 0, 2, 4)
+        look_up(0, 1)
+        quantise_w(1, 1, w_next[:], nc.scalar.copy)
+        quantise_w(2, 2, w_rest[:], nc.scalar.copy)
         product(1)
-        look_up(0, 1, 1)
-        look_up(0, 2, 1)
-        quantise_w(2, 2, w_rest[:, :, P:], nc.scalar.copy)
-        look_up(0, 3, 1)
+        look_up(0, 2, tag="w_packed1")
+        look_up(0, 3)
         product(2)
         product(3)
         for c in range(CORNERS):
-            look_up(1, c, 1)
+            look_up(1, c)
 
-        f_bank = psum.tile([P, P], F32)
+        f_bank = psum.tile([P, P], F32, tag="dv_bank0")
         nc.tensor.transpose(f_bank[:], f_rows[:], ident[:])
         weights = keep.tile([P, 2, BLOCKS, CORNERS], F32)
         fx_cols, fy_cols = f_bank[:, 0:4], f_bank[:, 4:8]
@@ -145,12 +150,19 @@ def tile_attend_gbilin_kernel(tc, xT, W, dyT, fx, fy, offs0, offs1, offs2, offs3
             for c, (scale, bias) in enumerate(signs):
                 nc.scalar.activation(out=weights[:, o, :, c], in_=f_cols, func=COPY, scale=scale, bias=bias)
 
-        for c in range(CORNERS):
-            look_up(2, c, 1)
-            look_up(3, c, 2 if c == CORNERS - 1 else 1)
-            row_sums(c, range(2) if c == CORNERS - 1 else range(BLOCKS))
-        nc.vector.tensor_reduce(out=sums[:, 2:4, CORNERS - 1], in_=acc_last[:], axis=AXIS_X, op=ADD)
+        for c in range(last):
+            look_up(2, c, tag=f"terms3{c - 2}" if c >= 2 else None)
+            look_up(3, c)
+            row_sums(c, range(BLOCKS))
+        look_up(2, last, 0, 2, tag="terms31")
+        look_up(3, last, 0, 2)
+        look_up(2, last, 2, 4)
+        look_up(3, last, 2, 3)
+        look_up(3, last, 3, 4)
 
+        nc.vector.tensor_reduce(out=sums[:, 0:2, last], in_=acc[last][:, 0:2, :], axis=AXIS_X, op=ADD)
+        for s in acc_late:
+            nc.vector.tensor_reduce(out=sums[:, s, last:], in_=acc_late[s][:], axis=AXIS_X, op=ADD)
         weighted = keep.tile([P, 2, BLOCKS, CORNERS], F32)
         nc.vector.tensor_tensor(weighted[:], weights[:], sums[:].unsqueeze(1).to_broadcast([P, 2, BLOCKS, CORNERS]), MULT)
         nc.vector.tensor_reduce(out=grads[:].rearrange("p (s r) -> p r s", r=32)[:, 0:2, :], in_=weighted[:], axis=AXIS_X, op=ADD)

from contextlib import ExitStack

import concourse.mybir as mybir
from concourse.masks import make_identity

F32 = mybir.dt.float32
BF16 = mybir.dt.bfloat16
U32 = mybir.dt.uint32
U16 = mybir.dt.uint16
U8 = mybir.dt.uint8
E4M3X4 = mybir.dt.float8_e4m3fn_x4
E5M2X4 = mybir.dt.float8_e5m2_x4
MULT = mybir.AluOpType.mult
ADD = mybir.AluOpType.add
COPY = mybir.ActivationFunctionType.Copy
AXIS_X = mybir.AxisListType.X

P = 128
PACK = 4
SAMPLES = 512
FEATURES = 512
PIXELS = 2048
CORNERS = 4
BLOCKS = 4
FLOPS = 2 * 512 * 512 * 512


def interleave(engine_copy, dst, src):
    engine_copy(out=dst.rearrange("p (c i) t -> p c t i", i=4), in_=src.rearrange("p t (c i) -> p c t i", i=4))


def tile_attend_gbilin_kernel(tc, xT, W, dyT, fx, fy, offs0, offs1, offs2, offs3, out_0, out_1):
    nc = tc.nc
    with ExitStack() as ctx:
        keep = ctx.enter_context(tc.tile_pool(name="keep", bufs=1))
        psum = ctx.enter_context(tc.psum_pool(name="psum", bufs=1))

        w_rows = W.rearrange("(p t) d -> p t d", t=PACK)
        dy_rows = dyT.rearrange("(p t) i -> p t i", t=PACK)
        lists = [keep.tile([P, SAMPLES // 16], U16, name=f"list{c}") for c in range(CORNERS)]
        image = [keep.tile([P, PIXELS], F32, name=f"image{b}") for b in range(BLOCKS)]
        w_head = keep.tile([P, PACK, P], F32)
        w_next = keep.tile([P, PACK, P], F32)
        w_rest = keep.tile([P, PACK, 2 * P], F32, tag="w_rest")
        dy_raw = [keep.tile([P, PACK, SAMPLES // 2], F32, name=f"dy_raw{h}") for h in range(2)]
        f_rows = keep.tile([P, P], F32)
        ident = keep.tile([P, P], F32)
        grads = keep.tile([P, P], F32, align_bytes=64)

        nc.sync.dma_start(out=w_head[:], in_=w_rows[:, :, 0:P])
        for h in range(2):
            nc.sync.dma_start(out=dy_raw[h][:], in_=dy_rows[:, :, h * 256:(h + 1) * 256])
        nc.sync.dma_start(lists[0][:], offs0)
        nc.sync.dma_start(out=image[0][:], in_=xT[0:P, :])
        nc.sync.dma_start(lists[1][:], offs1)
        nc.sync.dma_start(out=w_next[:], in_=w_rows[:, :, P:2 * P])
        nc.sync.dma_start(lists[2][:], offs2)
        nc.sync.dma_start(lists[3][:], offs3)
        nc.sync.dma_start(out=w_rest[:], in_=w_rows[:, :, 2 * P:])
        for b in range(1, BLOCKS):
            nc.sync.dma_start(out=image[b][:], in_=xT[b * P:(b + 1) * P, :])
        nc.gpsimd.memset(f_rows[:], 0.0)
        nc.gpsimd.memset(grads[:], 0.0)
        make_identity(nc, ident[:])
        nc.sync.dma_start(out=f_rows[0:4, :], in_=fx.rearrange("(s p) o -> s (p o)", p=P))
        nc.sync.dma_start(out=f_rows[4:8, :], in_=fy.rearrange("(s p) o -> s (p o)", p=P))

        w_codes = {}
        w_scales = {}

        def quantise_w(first, count, raw, engine_copy):
            packed = keep.tile([P, count * P, PACK], BF16, name=f"w_packed{first}", tag=f"w_packed{first}", align_bytes=64)
            codes = keep.tile([P, count * P], U32, name=f"w_codes{first}", align_bytes=64)
            scales = keep.tile([P, count * P], U8, name=f"w_scales{first}", align_bytes=64)
            interleave(engine_copy, packed[:], raw)
            nc.vector.quantize_mx(out=codes[:].bitcast(E4M3X4), scales=scales[:], in_=packed[:].rearrange("p d t -> p (d t)"))
            for j in range(count):
                w_codes[first + j] = codes[:, j * P:(j + 1) * P]
                w_scales[first + j] = scales[:, j * P:(j + 1) * P]

        quantise_w(0, 1, w_head[:], nc.scalar.copy)
        dy_codes = keep.tile([P, SAMPLES], U32, align_bytes=64)
        dy_scales = keep.tile([P, SAMPLES], U8, align_bytes=64)
        split = 176
        for h in range(2):
            packed = keep.tile([P, 256, PACK], BF16, name=f"dy_packed{h}", align_bytes=64)
            interleave(nc.vector.tensor_copy, packed[:, 0:split, :], dy_raw[h][:, :, 0:split])
            interleave(nc.scalar.copy, packed[:, split:, :], dy_raw[h][:, :, split:])
            cols = slice(h * 256, (h + 1) * 256)
            nc.vector.quantize_mx(out=dy_codes[:, cols].bitcast(E5M2X4), scales=dy_scales[:, cols], in_=packed[:].rearrange("p i t -> p (i t)"))

        dv = {}

        def product(b, pieces=1):
            bank = psum.tile([P, SAMPLES], F32, name="dv_bank", tag=f"dv_bank{b % 2}")
            nc.tensor.matmul_mx(out=bank[:], lhsT=w_codes[b].bitcast(E4M3X4), lhsT_scale=w_scales[b],
                                rhs=dy_codes[:].bitcast(E5M2X4), rhs_scale=dy_scales[:], start=True, stop=True)
            dv[b] = keep.tile([P, SAMPLES], F32, name=f"dv{b}", tag="w_rest" if b == 1 else f"dv{b}")
            width = SAMPLES // pieces
            for h in range(pieces):
                nc.scalar.copy(out=dv[b][:, h * width:(h + 1) * width], in_=bank[:, h * width:(h + 1) * width])

        sums = keep.tile([P, BLOCKS, CORNERS], F32)
        last = CORNERS - 1
        acc = [psum.tile([P, BLOCKS, P], F32, name=f"acc{c}") for c in range(CORNERS)]
        acc_late = {s: psum.tile([P, P], F32, name=f"acc_late{s}") for s in (2, 3)}
        terms = {}

        def acc_of(c, s):
            if c == last and s in acc_late:
                return acc_late[s][:], True, True
            return acc[c][:, s, :], s == 0, s == (1 if c == last else 3)

        def look_up(b, c, s_from=0, s_to=BLOCKS, tag=None):
            if (b, c) not in terms:
                terms[b, c] = keep.tile([P, SAMPLES], F32, name=f"terms{b}{c}", tag=tag or f"terms{b}{c}", align_bytes=64)
            cols = slice(s_from * P, s_to * P)
            offsets = lists[c][:, s_from * P // 16:s_to * P // 16]
            nc.vector.tensor_tensor(terms[b, c][:, cols], image[b][:].indirect(offsets), dv[b][:, cols], MULT)
            for s in range(s_from, s_to):
                target, opens, closes = acc_of(c, s)
                nc.tensor.matmul(out=target, lhsT=terms[b, c][:, s * P:(s + 1) * P], rhs=ident[:], is_transpose=True,
                                 start=(b == 0 and opens), stop=(b == BLOCKS - 1 and closes))

        def row_sums(c, blocks):
            spent = keep.tile([P, BLOCKS, P], F32, name=f"spent{c}")
            for s in blocks:
                nc.scalar.activation(out=spent[:, s, :], in_=acc[c][:, s, :], func=COPY, accum_out=sums[:, s, c:c + 1])

        product(0, 2)
        look_up(0, 0, 0, 2)
        look_up(0, 0, 2, 4)
        look_up(0, 1)
        quantise_w(1, 1, w_next[:], nc.scalar.copy)
        quantise_w(2, 2, w_rest[:], nc.scalar.copy)
        product(1)
        look_up(0, 2, tag="w_packed1")
        look_up(0, 3)
        product(2)
        product(3)
        for c in range(CORNERS):
            look_up(1, c)

        f_bank = psum.tile([P, P], F32, tag="dv_bank0")
        nc.tensor.transpose(f_bank[:], f_rows[:], ident[:])
        weights = keep.tile([P, 2, BLOCKS, CORNERS], F32)
        fx_cols, fy_cols = f_bank[:, 0:4], f_bank[:, 4:8]
        for o, f_cols, signs in ((0, fy_cols, ((1.0, -1.0), (-1.0, 1.0), (-1.0, 0.0), (1.0, 0.0))),
                                 (1, fx_cols, ((1.0, -1.0), (-1.0, 0.0), (-1.0, 1.0), (1.0, 0.0)))):
            for c, (scale, bias) in enumerate(signs):
                nc.scalar.activation(out=weights[:, o, :, c], in_=f_cols, func=COPY, scale=scale, bias=bias)

        for c in range(last):
            look_up(2, c, tag=f"terms3{c - 2}" if c >= 2 else None)
            look_up(3, c)
            row_sums(c, range(BLOCKS))
        look_up(2, last, 0, 2, tag="terms31")
        look_up(3, last, 0, 2)
        look_up(2, last, 2, 4)
        look_up(3, last, 2, 3)
        look_up(3, last, 3, 4)

        nc.vector.tensor_reduce(out=sums[:, 0:2, last], in_=acc[last][:, 0:2, :], axis=AXIS_X, op=ADD)
        for s in acc_late:
            nc.vector.tensor_reduce(out=sums[:, s, last:], in_=acc_late[s][:], axis=AXIS_X, op=ADD)
        weighted = keep.tile([P, 2, BLOCKS, CORNERS], F32)
        nc.vector.tensor_tensor(weighted[:], weights[:], sums[:].unsqueeze(1).to_broadcast([P, 2, BLOCKS, CORNERS]), MULT)
        nc.vector.tensor_reduce(out=grads[:].rearrange("p (s r) -> p r s", r=32)[:, 0:2, :], in_=weighted[:], axis=AXIS_X, op=ADD)
        turned = keep.tile([P, P], F32, align_bytes=64)
        nc.vector.transpose(turned[:], grads[:])
        nc.sync.dma_start(out=out_0.rearrange("o (s q r) -> (o q) s r", s=BLOCKS, q=4),
                          in_=turned[0:P:32, :].rearrange("q (s r) -> q s r", r=32))
        nc.scalar.dma_start(out=out_1.rearrange("o (s q r) -> (o q) s r", s=BLOCKS, q=4),
                            in_=turned[1:P:32, :].rearrange("q (s r) -> q s r", r=32))
